import numpy as np, ml_dtypes
CORES = [4,20,36,52,68,84,100,116,132,148,164,180,196,212,228,244]
N = 16
K, F = 4, 64
def setup_inputs(rng):
    return {"gr": rng.standard_normal((N, K, 128, N * F), dtype=np.float32).astype(ml_dtypes.bfloat16)}
def setup_inputs_big(rng):
    d = setup_inputs(rng)
    for k in ("gr",): d[k] = (d[k].astype(np.float32) * 1048576.0).astype(d[k].dtype)
    return d
def setup_inputs_small(rng):
    d = setup_inputs(rng)
    for k in ("gr",): d[k] = (d[k].astype(np.float32) * (1 / 1048576.0)).astype(d[k].dtype)
    return d
def reference(gr):
    s = gr.astype(np.float64).sum(axis=(0, 1))
    return {"y": np.stack([s[:, F * r:F * r + F] for r in range(N)]).astype(np.float32 if gr.dtype != np.float64 else np.float64)}

@@ -1,0 +1,194 @@
+from concourse.bass import DstId, RemoteDMATransfer
+from concourse.mybir import AluOpType
+
+N, K, F = 16, 4, 64
+SIM_CORES = 256
+HALF = N // 2 * F
+PAIR = 2 * F
+NP = HALF // PAIR
+
+SCRATCH = {
+    "tab0": ("sbuf", [128, N * F], "bfloat16"),
+    "tab1": ("sbuf", [128, N * F], "bfloat16"),
+    "tab2": ("sbuf", [128, N * F], "bfloat16"),
+    "tab3": ("sbuf", [128, N * F], "bfloat16"),
+    "stage": ("sbuf", [128, N * F], "float32"),
+    "land": ("sbuf", [128, N * F], "float32"),
+    "seed": ("sbuf", [128, 33 * 32], "bfloat16"),
+    "idb": ("sbuf", [128, 128], "bfloat16"),
+    "idf": ("sbuf", [128, 128], "float32"),
+    "res": ("sbuf", [128, F], "float32"),
+    "psa": ("psum", [128, 512], "float32"),
+    "psb": ("psum", [128, 512], "float32"),
+    "fin": ("psum", [128, 512], "float32"),
+}
+SEMAPHORES = (["fillz", "fill", "idd", "idc1", "idc2", "idc3", "pe0", "pe1", "st0", "st1", "std", "h0", "h1", "sent",
+               "pefin", "vfin", "ydone"]
+              + ["l%d%d" % (c, k) for c in range(2) for k in range(K)]
+              + ["a%d" % s for s in range(N)])
+
+
+def _bits(mask):
+    return [e for e in range(mask.bit_length()) if (mask >> e) & 1]
+
+
+def _mask(engines):
+    m = 0
+    for e in engines:
+        m |= 1 << e
+    return m
+
+
+def _helpers(owner, topo):
+    chip = [c for c in range(SIM_CORES)
+            if c != owner and topo.host(c) == topo.host(owner) and topo.chip(c) == topo.chip(owner)]
+    same = [c for c in chip if topo.die(c) == topo.die(owner)]
+    other = [c for c in chip if topo.die(c) != topo.die(owner)]
+    return [same[0], other[0], same[1], other[1]]
+
+
+def _plan(r):
+    h, q = r // (N // 2), (r % (N // 2)) // 2
+    first = [((j + r) % NP, (1 - h) * (N // 2) + 2 * j) for j in range(NP)]
+    late_helper = {1: 0, 2: 1, 3: 3}
+    second = [(late_helper[(j - q) % NP], h * (N // 2) + 2 * j) for j in range(NP) if j != q]
+    return first, second
+
+
+def _helper_program(g, core, T, topo, owner, idx):
+    r = T.rank_of(owner)
+    sent = 0
+    for phase, pairs in enumerate(_plan(r)):
+        for hi, d0 in pairs:
+            if hi != idx:
+                continue
+            g.wait_ge(T.sem["h%d" % phase], 4)
+            trs = []
+            for t in range(2):
+                d = d0 + t
+                dst = T.cores[d]
+                rid, pid = topo.addr(dst, core)
+                eng = _bits(topo.mask(core, dst))[t::2]
+                trs.append(RemoteDMATransfer(dst_ids=[DstId(rid=rid, pnc=pid)], dma_engine_mask=_mask(eng),
+                                             remote_sem=T.sem["a%d" % r],
+                                             src=T.stage[:, d * F:(d + 1) * F], dst=T.land[:, r * F:(r + 1) * F]))
+                sent += len(eng)
+            g.remote_dma_fused(trs, local_sem=T.sem.sent)
+    g.wait_ge(T.sem.sent, sent)
+
+
+def rank_program(g, core, T, topo):
+    owners = [c for c in T.cores if topo.host(c) == topo.host(core) and topo.chip(c) == topo.chip(core)]
+    if not owners:
+        return
+    owner = owners[0]
+    helpers = _helpers(owner, topo)
+    if core != owner:
+        if core in helpers:
+            _helper_program(g, core, T, topo, owner, helpers.index(core))
+        return
+
+    r = T.rank_of(core)
+    h = r // (N // 2)
+    q = (r % (N // 2)) // 2
+    partner = r ^ 1
+    tab = [T.tab0, T.tab1, T.tab2, T.tab3]
+    col0 = [(1 - h) * HALF, h * HALF]
+    ps = [T.psa, T.psb]
+    v, pe = g.vector, g.tensor
+    first, second = _plan(r)
+
+    def load(qu, c, k):
+        qu.dma_start(tab[k][:, col0[c]:col0[c] + HALF], T.gr[k, :, col0[c]:col0[c] + HALF]).then_inc(
+            T.sem["l%d%d" % (c, k)], 16)
+
+    load(g.sync, 0, 0)
+    v.memset(T.seed[0:1, :], 0.0).then_inc(T.sem.fillz, 1)
+    v.memset(T.idb[:, :], 0.0).then_inc(T.sem.fill, 1)
+    v.wait_ge(T.sem.fillz, 1)
+    v.memset(T.seed[0:1, 0:33 * 32:33], 1.0).then_inc(T.sem.fill, 1)
+    g.scalar.wait_ge(T.sem.fill, 2)
+    g.scalar.dma_start(T.idb[0:33, 0:32], T.seed[0:1, :]).then_inc(T.sem.idd, 16)
+    g.sync.wait_ge(T.sem.fill, 2)
+    for c, k in ((0, 1), (0, 2), (0, 3), (1, 0), (1, 1), (1, 2), (1, 3)):
+        load(g.sync if k % 2 else g.scalar, c, k)
+
+    v.wait_ge(T.sem.idd, 16)
+    v.tensor_copy(T.idb[32:64, 32:64], T.idb[0:32, 0:32]).then_inc(T.sem.idc1, 1)
+    v.wait_ge(T.sem.idc1, 1)
+    v.tensor_copy(T.idb[64:128, 64:128], T.idb[0:64, 0:64]).then_inc(T.sem.idc2, 1)
+    v.wait_ge(T.sem.idc2, 1)
+    v.tensor_copy(T.idf[:, :], T.idb[:, :]).then_inc(T.sem.idc3, 1)
+
+    pe.wait_ge(T.sem.idc2, 1)
+    for c in range(2):
+        for k in range(K - 1):
+            pe.wait_ge(T.sem["l%d%d" % (c, k)], 16)
+            mm = pe.matmul(ps[c][:, :], T.idb[:, :], tab[k][:, col0[c]:col0[c] + HALF], k == 0, k == K - 2)
+        mm.then_inc(T.sem["pe%d" % c], 1)
+
+    def fold(c, lo, hi, sem):
+        a = col0[c]
+        v.tensor_tensor(T.stage[:, a + lo:a + hi], ps[c][:, lo:hi], tab[K - 1][:, a + lo:a + hi],
+                        AluOpType.add).then_inc(sem, 1)
+
+    v.wait_ge(T.sem.pe0, 1)
+    v.wait_ge(T.sem["l0%d" % (K - 1)], 16)
+    fold(0, 0, HALF, T.sem.st0)
+    v.wait_ge(T.sem.pe1, 1)
+    v.wait_ge(T.sem["l1%d" % (K - 1)], 16)
+    n_st1 = 0
+    for lo, hi in ((0, q * PAIR), ((q + 1) * PAIR, HALF)):
+        if hi > lo:
+            fold(1, lo, hi, T.sem.st1)
+            n_st1 += 1
+    pl = partner * F - col0[1]
+    fold(1, pl, pl + F, T.sem.std)
+
+    all_eng = _bits(topo.mask(core, helpers[0]))
+    off_eng = _bits(topo.mask(core, T.cores[partner]))
+    rest = [e for e in all_eng if e not in off_eng]
+    late_eng = {0: off_eng[1::2], 1: rest[0::2], 3: rest[1::2]}
+    sent = 0
+
+    def to_helpers(pairs, engines, sem):
+        trs, n = [], 0
+        for hi, d0 in pairs:
+            rid, pid = topo.addr(helpers[hi], core)
+            ap = T.stage[:, d0 * F:d0 * F + PAIR]
+            trs.append(RemoteDMATransfer(dst_ids=[DstId(rid=rid, pnc=pid)], dma_engine_mask=_mask(engines[hi]),
+                                         remote_sem=sem, src=ap, dst=ap))
+            n += len(engines[hi])
+        g.remote_dma_fused(trs, local_sem=T.sem.sent)
+        return n
+
+    g.wait_ge(T.sem.st0, 1)
+    sent += to_helpers(first, {i: all_eng[i::NP] for i in range(NP)}, T.sem.h0)
+    g.wait_ge(T.sem.st1, n_st1)
+    sent += to_helpers(second, late_eng, T.sem.h1)
+    g.wait_ge(T.sem.std, 1)
+    rid, pid = topo.addr(T.cores[partner], core)
+    g.remote_dma(T.land[:, r * F:(r + 1) * F], T.stage[:, partner * F:(partner + 1) * F], T.sem["a%d" % r], T.sem.sent,
+                 pid, rid, _mask(off_eng[0::2]))
+    sent += len(off_eng[0::2])
+
+    pe.wait_ge(T.sem["l1%d" % (K - 1)], 16)
+    for k in range(K):
+        pe.matmul(T.fin[:, 0:F], T.idb[:, :], tab[k][:, r * F:(r + 1) * F], k == 0, False)
+    early = [(1 - h) * (N // 2) + (r + i) % (N // 2) for i in range(N // 2)]
+    late = [h * (N // 2) + 2 * ((q - o) % NP) + t for o in (1, 2, 3) for t in range(2)]
+    order = early + [partner] + late
+    pe.wait_ge(T.sem.idc3, 1)
+    for i, s in enumerate(order[:-1]):
+        pe.wait_ge(T.sem["a%d" % s], 4)
+        mm = pe.matmul(T.fin[:, 0:F], T.idf[:, :], T.land[:, s * F:(s + 1) * F], False, i == len(order) - 2)
+    mm.then_inc(T.sem.pefin, 1)
+
+    last = order[-1]
+    v.wait_ge(T.sem.pefin, 1)
+    v.wait_ge(T.sem["a%d" % last], 4)
+    v.tensor_tensor(T.res[:, :], T.fin[:, 0:F], T.land[:, last * F:(last + 1) * F], AluOpType.add).then_inc(T.sem.vfin, 1)
+    g.sync.wait_ge(T.sem.vfin, 1)
+    g.sync.dma_start(T.y[:, :], T.res[:, :]).then_inc(T.sem.ydone, 16)
+    g.sync.wait_ge(T.sem.ydone, 16)
+    g.wait_ge(T.sem.sent, sent)

@@ -3,9 +3,10 @@ from concourse.mybir import AluOpType
 
 N, K, F = 16, 4, 64
 SIM_CORES = 256
-HALF = N // 2 * F
+HN = N // 2
+QN = N // 4
 PAIR = 2 * F
-NP = HALF // PAIR
+NP = HN // 2
 
 SCRATCH = {
     "tab0": ("sbuf", [128, N * F], "bfloat16"),
@@ -17,14 +18,16 @@ SCRATCH = {
     "seed": ("sbuf", [128, 33 * 32], "bfloat16"),
     "idb": ("sbuf", [128, 128], "bfloat16"),
     "idf": ("sbuf", [128, 128], "float32"),
+    "two": ("sbuf", [128, F], "float32"),
     "res": ("sbuf", [128, F], "float32"),
-    "psa": ("psum", [128, 512], "float32"),
-    "psb": ("psum", [128, 512], "float32"),
+    "ps0": ("psum", [128, 512], "float32"),
+    "ps1": ("psum", [128, 512], "float32"),
+    "ps2": ("psum", [128, 512], "float32"),
     "fin": ("psum", [128, 512], "float32"),
 }
-SEMAPHORES = (["fillz", "fill", "idd", "idc1", "idc2", "idc3", "pe0", "pe1", "st0", "st1", "std", "h0", "h1", "sent",
-               "pefin", "vfin", "ydone"]
-              + ["l%d%d" % (c, k) for c in range(2) for k in range(K)]
+SEMAPHORES = (["fillz", "fill", "idd", "idc1", "idc2", "idc3", "pe0", "pe1", "pe2", "st0", "st1", "st2", "std", "stp",
+               "h0", "h1", "h2", "sent", "pefin", "vtwo", "vfin", "ydone"]
+              + ["l%d%d" % (c, k) for c in range(3) for k in range(K)]
               + ["a%d" % s for s in range(N)])
 
 
@@ -47,33 +50,58 @@ def _helpers(owner, topo):
     return [same[0], other[0], same[1], other[1]]
 
 
-def _plan(r):
-    h, q = r // (N // 2), (r % (N // 2)) // 2
-    first = [((j + r) % NP, (1 - h) * (N // 2) + 2 * j) for j in range(NP)]
-    late_helper = {1: 0, 2: 1, 3: 3}
-    second = [(late_helper[(j - q) % NP], h * (N // 2) + 2 * j) for j in range(NP) if j != q]
-    return first, second
+def _quarters(r):
+    base = (1 - r // HN) * HN
+    return [base + (r % 2) * QN, base + (1 - r % 2) * QN]
+
+
+def _singles(r, c):
+    return [((j + r // 2) % QN, _quarters(r)[c] + j) for j in range(QN)]
+
+
+def _pairs(r):
+    h, q = r // HN, (r % HN) // 2
+    return [(hi, h * HN + 2 * ((q + o) % NP)) for o, hi in ((2, 1), (3, 3))]
+
+
+def _transfer(T, topo, core, dst, engines, sem, src, out):
+    rid, pid = topo.addr(dst, core)
+    return RemoteDMATransfer(dst_ids=[DstId(rid=rid, pnc=pid)], dma_engine_mask=_mask(engines), remote_sem=sem,
+                             src=src, dst=out)
+
+
+def _block(g, core, T, topo, r, d):
+    eng = _bits(topo.mask(core, T.cores[d]))
+    rid, pid = topo.addr(T.cores[d], core)
+    g.remote_dma(T.land[:, r * F:(r + 1) * F], T.stage[:, d * F:(d + 1) * F], T.sem["a%d" % r], T.sem.sent,
+                 pid, rid, _mask(eng))
+    return len(eng)
+
+
+def _blocks(g, core, T, topo, r, d0):
+    trs, n = [], 0
+    for t in range(2):
+        d = d0 + t
+        eng = _bits(topo.mask(core, T.cores[d]))[t::2]
+        trs.append(_transfer(T, topo, core, T.cores[d], eng, T.sem["a%d" % r],
+                             T.stage[:, d * F:(d + 1) * F], T.land[:, r * F:(r + 1) * F]))
+        n += len(eng)
+    g.remote_dma_fused(trs, local_sem=T.sem.sent)
+    return n
 
 
 def _helper_program(g, core, T, topo, owner, idx):
     r = T.rank_of(owner)
+    n_on = len(_bits(topo.mask(owner, core)))
     sent = 0
-    for phase, pairs in enumerate(_plan(r)):
-        for hi, d0 in pairs:
-            if hi != idx:
-                continue
-            g.wait_ge(T.sem["h%d" % phase], 4)
-            trs = []
-            for t in range(2):
-                d = d0 + t
-                dst = T.cores[d]
-                rid, pid = topo.addr(dst, core)
-                eng = _bits(topo.mask(core, dst))[t::2]
-                trs.append(RemoteDMATransfer(dst_ids=[DstId(rid=rid, pnc=pid)], dma_engine_mask=_mask(eng),
-                                             remote_sem=T.sem["a%d" % r],
-                                             src=T.stage[:, d * F:(d + 1) * F], dst=T.land[:, r * F:(r + 1) * F]))
-                sent += len(eng)
-            g.remote_dma_fused(trs, local_sem=T.sem.sent)
+    for c in range(2):
+        d = [d for hi, d in _singles(r, c) if hi == idx][0]
+        g.wait_ge(T.sem["h%d" % c], n_on // QN)
+        sent += _block(g, core, T, topo, r, d)
+    for hi, d0 in _pairs(r):
+        if hi == idx:
+            g.wait_ge(T.sem.h2, n_on // 2)
+            sent += _blocks(g, core, T, topo, r, d0)
     g.wait_ge(T.sem.sent, sent)
 
 
@@ -89,20 +117,23 @@ def rank_program(g, core, T, topo):
         return
 
     r = T.rank_of(core)
-    h = r // (N // 2)
-    q = (r % (N // 2)) // 2
+    h = r // HN
+    q = (r % HN) // 2
     partner = r ^ 1
     tab = [T.tab0, T.tab1, T.tab2, T.tab3]
-    col0 = [(1 - h) * HALF, h * HALF]
-    ps = [T.psa, T.psb]
+    qs = _quarters(r)
+    col0 = [qs[0] * F, qs[1] * F, h * HN * F]
+    wid = [QN * F, QN * F, HN * F]
+    ps = [T.ps0, T.ps1, T.ps2]
     v, pe = g.vector, g.tensor
-    first, second = _plan(r)
+    near = h * HN + 2 * ((q + 1) % NP)
 
     def load(qu, c, k):
-        qu.dma_start(tab[k][:, col0[c]:col0[c] + HALF], T.gr[k, :, col0[c]:col0[c] + HALF]).then_inc(
+        qu.dma_start(tab[k][:, col0[c]:col0[c] + wid[c]], T.gr[k, :, col0[c]:col0[c] + wid[c]]).then_inc(
             T.sem["l%d%d" % (c, k)], 16)
 
-    load(g.sync, 0, 0)
+    for k in range(K):
+        load(g.sync, 0, k)
     v.memset(T.seed[0:1, :], 0.0).then_inc(T.sem.fillz, 1)
     v.memset(T.idb[:, :], 0.0).then_inc(T.sem.fill, 1)
     v.wait_ge(T.sem.fillz, 1)
@@ -110,84 +141,90 @@ def rank_program(g, core, T, topo):
     g.scalar.wait_ge(T.sem.fill, 2)
     g.scalar.dma_start(T.idb[0:33, 0:32], T.seed[0:1, :]).then_inc(T.sem.idd, 16)
     g.sync.wait_ge(T.sem.fill, 2)
-    for c, k in ((0, 1), (0, 2), (0, 3), (1, 0), (1, 1), (1, 2), (1, 3)):
-        load(g.sync if k % 2 else g.scalar, c, k)
+    for c in (1, 2):
+        for k in range(K):
+            load(g.sync if k % 2 else g.scalar, c, k)
 
     v.wait_ge(T.sem.idd, 16)
     v.tensor_copy(T.idb[32:64, 32:64], T.idb[0:32, 0:32]).then_inc(T.sem.idc1, 1)
     v.wait_ge(T.sem.idc1, 1)
     v.tensor_copy(T.idb[64:128, 64:128], T.idb[0:64, 0:64]).then_inc(T.sem.idc2, 1)
-    v.wait_ge(T.sem.idc2, 1)
-    v.tensor_copy(T.idf[:, :], T.idb[:, :]).then_inc(T.sem.idc3, 1)
 
     pe.wait_ge(T.sem.idc2, 1)
-    for c in range(2):
+    for c in range(3):
         for k in range(K - 1):
             pe.wait_ge(T.sem["l%d%d" % (c, k)], 16)
-            mm = pe.matmul(ps[c][:, :], T.idb[:, :], tab[k][:, col0[c]:col0[c] + HALF], k == 0, k == K - 2)
+            mm = pe.matmul(ps[c][:, 0:wid[c]], T.idb[:, :], tab[k][:, col0[c]:col0[c] + wid[c]], k == 0, k == K - 2)
         mm.then_inc(T.sem["pe%d" % c], 1)
 
-    def fold(c, lo, hi, sem):
-        a = col0[c]
-        v.tensor_tensor(T.stage[:, a + lo:a + hi], ps[c][:, lo:hi], tab[K - 1][:, a + lo:a + hi],
+    def fold(c, a, n, sem):
+        v.tensor_tensor(T.stage[:, a:a + n], ps[c][:, a - col0[c]:a - col0[c] + n], tab[K - 1][:, a:a + n],
                         AluOpType.add).then_inc(sem, 1)
 
-    v.wait_ge(T.sem.pe0, 1)
-    v.wait_ge(T.sem["l0%d" % (K - 1)], 16)
-    fold(0, 0, HALF, T.sem.st0)
-    v.wait_ge(T.sem.pe1, 1)
-    v.wait_ge(T.sem["l1%d" % (K - 1)], 16)
-    n_st1 = 0
-    for lo, hi in ((0, q * PAIR), ((q + 1) * PAIR, HALF)):
-        if hi > lo:
-            fold(1, lo, hi, T.sem.st1)
-            n_st1 += 1
-    pl = partner * F - col0[1]
-    fold(1, pl, pl + F, T.sem.std)
+    for c in range(2):
+        v.wait_ge(T.sem["pe%d" % c], 1)
+        v.wait_ge(T.sem["l%d%d" % (c, K - 1)], 16)
+        fold(c, col0[c], wid[c], T.sem["st%d" % c])
+        if c == 0:
+            v.wait_ge(T.sem.idc2, 1)
+            v.tensor_copy(T.idf[:, :], T.idb[:, :]).then_inc(T.sem.idc3, 1)
+    v.wait_ge(T.sem.pe2, 1)
+    v.wait_ge(T.sem["l2%d" % (K - 1)], 16)
+    for hi, d0 in _pairs(r):
+        fold(2, d0 * F, PAIR, T.sem.st2)
+    fold(2, near * F, PAIR, T.sem.std)
+    fold(2, partner * F, F, T.sem.stp)
 
     all_eng = _bits(topo.mask(core, helpers[0]))
-    off_eng = _bits(topo.mask(core, T.cores[partner]))
-    rest = [e for e in all_eng if e not in off_eng]
-    late_eng = {0: off_eng[1::2], 1: rest[0::2], 3: rest[1::2]}
     sent = 0
 
-    def to_helpers(pairs, engines, sem):
+    def to_helpers(items, width, deal, sem):
         trs, n = [], 0
-        for hi, d0 in pairs:
-            rid, pid = topo.addr(helpers[hi], core)
-            ap = T.stage[:, d0 * F:d0 * F + PAIR]
-            trs.append(RemoteDMATransfer(dst_ids=[DstId(rid=rid, pnc=pid)], dma_engine_mask=_mask(engines[hi]),
-                                         remote_sem=sem, src=ap, dst=ap))
-            n += len(engines[hi])
+        for i, (hi, d0) in enumerate(items):
+            eng = all_eng[(hi if deal else i)::len(items)]
+            ap = T.stage[:, d0 * F:d0 * F + width]
+            trs.append(_transfer(T, topo, core, helpers[hi], eng, sem, ap, ap))
+            n += len(eng)
         g.remote_dma_fused(trs, local_sem=T.sem.sent)
         return n
 
-    g.wait_ge(T.sem.st0, 1)
-    sent += to_helpers(first, {i: all_eng[i::NP] for i in range(NP)}, T.sem.h0)
-    g.wait_ge(T.sem.st1, n_st1)
-    sent += to_helpers(second, late_eng, T.sem.h1)
+    for c in range(2):
+        g.wait_ge(T.sem["st%d" % c], 1)
+        sent += to_helpers(_singles(r, c), F, True, T.sem["h%d" % c])
+    g.wait_ge(T.sem.st2, 2)
+    sent += to_helpers(_pairs(r), PAIR, False, T.sem.h2)
     g.wait_ge(T.sem.std, 1)
-    rid, pid = topo.addr(T.cores[partner], core)
-    g.remote_dma(T.land[:, r * F:(r + 1) * F], T.stage[:, partner * F:(partner + 1) * F], T.sem["a%d" % r], T.sem.sent,
-                 pid, rid, _mask(off_eng[0::2]))
-    sent += len(off_eng[0::2])
+    sent += _blocks(g, core, T, topo, r, near)
+    g.wait_ge(T.sem.stp, 1)
+    sent += _block(g, core, T, topo, r, partner)
 
-    pe.wait_ge(T.sem["l1%d" % (K - 1)], 16)
+    def arrived(qu, s):
+        n = len(_bits(topo.mask(T.cores[s], core)))
+        qu.wait_ge(T.sem["a%d" % s], n if (s == partner or s // HN != h) else n // 2)
+
+    def slot(s):
+        return T.land[:, s * F:(s + 1) * F]
+
+    pe.wait_ge(T.sem["l2%d" % (K - 1)], 16)
     for k in range(K):
         pe.matmul(T.fin[:, 0:F], T.idb[:, :], tab[k][:, r * F:(r + 1) * F], k == 0, False)
-    early = [(1 - h) * (N // 2) + (r + i) % (N // 2) for i in range(N // 2)]
-    late = [h * (N // 2) + 2 * ((q - o) % NP) + t for o in (1, 2, 3) for t in range(2)]
-    order = early + [partner] + late
+    others = [(1 - h) * HN + (r + i) % HN for i in range(HN)]
+    mine = (r // QN) * QN
+    early = [s for s in others if _quarters(s)[0] == mine] + [s for s in others if _quarters(s)[0] != mine]
+    late = [h * HN + 2 * ((q - o) % NP) + t for o in (1, 2, 3) for t in range(2)]
+    order = early + late[0:2] + [partner] + late[2:]
     pe.wait_ge(T.sem.idc3, 1)
-    for i, s in enumerate(order[:-1]):
-        pe.wait_ge(T.sem["a%d" % s], 4)
-        mm = pe.matmul(T.fin[:, 0:F], T.idf[:, :], T.land[:, s * F:(s + 1) * F], False, i == len(order) - 2)
+    for i, s in enumerate(order[:-2]):
+        arrived(pe, s)
+        mm = pe.matmul(T.fin[:, 0:F], T.idf[:, :], slot(s), False, i == len(order) - 3)
     mm.then_inc(T.sem.pefin, 1)
 
-    last = order[-1]
+    arrived(v, order[-2])
+    arrived(v, order[-1])
+    v.tensor_tensor(T.two[:, :], slot(order[-2]), slot(order[-1]), AluOpType.add).then_inc(T.sem.vtwo, 1)
+    v.wait_ge(T.sem.vtwo, 1)
     v.wait_ge(T.sem.pefin, 1)
-    v.wait_ge(T.sem["a%d" % last], 4)
-    v.tensor_tensor(T.res[:, :], T.fin[:, 0:F], T.land[:, last * F:(last + 1) * F], AluOpType.add).then_inc(T.sem.vfin, 1)
+    v.tensor_tensor(T.res[:, :], T.fin[:, 0:F], T.two[:, :], AluOpType.add).then_inc(T.sem.vfin, 1)
     g.sync.wait_ge(T.sem.vfin, 1)
     g.sync.dma_start(T.y[:, :], T.res[:, :]).then_inc(T.sem.ydone, 16)
     g.sync.wait_ge(T.sem.ydone, 16)

@@ -7,6 +7,7 @@ HN = N // 2
 QN = N // 4
 PAIR = 2 * F
 NP = HN // 2
+SL = F // QN
 
 SCRATCH = {
     "tab0": ("sbuf", [128, N * F], "bfloat16"),
@@ -18,6 +19,8 @@ SCRATCH = {
     "seed": ("sbuf", [128, 33 * 32], "bfloat16"),
     "idb": ("sbuf", [128, 128], "bfloat16"),
     "idf": ("sbuf", [128, 128], "float32"),
+    "oa": ("sbuf", [128, F], "float32"),
+    "ob": ("sbuf", [128, F], "float32"),
     "two": ("sbuf", [128, F], "float32"),
     "res": ("sbuf", [128, F], "float32"),
     "ps0": ("psum", [128, 512], "float32"),
@@ -26,8 +29,9 @@ SCRATCH = {
     "fin": ("psum", [128, 512], "float32"),
 }
 SEMAPHORES = (["fillz", "fill", "idd", "idc1", "idc2", "idc3", "pe0", "pe1", "pe2", "st0", "st1", "st2", "std", "stp",
-               "h0", "h1", "h2", "sent", "pefin", "vtwo", "vfin", "ydone"]
+               "h0", "h1", "h2", "ho", "vo", "sto", "sent", "pefin", "vtwo", "vfin", "ydone"]
               + ["l%d%d" % (c, k) for c in range(3) for k in range(K)]
+              + ["lo%d" % k for k in range(K)]
               + ["a%d" % s for s in range(N)])
 
 
@@ -55,8 +59,12 @@ def _quarters(r):
     return [base + (r % 2) * QN, base + (1 - r % 2) * QN]
 
 
+def _opener(r):
+    return _quarters(r)[0]
+
+
 def _singles(r, c):
-    return [((j + r // 2) % QN, _quarters(r)[c] + j) for j in range(QN)]
+    return [((j + r // 2) % QN, _quarters(r)[c] + j) for j in range(1 if c == 0 else 0, QN)]
 
 
 def _pairs(r):
@@ -94,10 +102,17 @@ def _helper_program(g, core, T, topo, owner, idx):
     r = T.rank_of(owner)
     n_on = len(_bits(topo.mask(owner, core)))
     sent = 0
+    d = _opener(r)
+    eng = _bits(topo.mask(core, T.cores[d]))
+    rid, pid = topo.addr(T.cores[d], core)
+    g.wait_ge(T.sem.ho, n_on // QN)
+    g.remote_dma(T.land[:, r * F + idx * SL:r * F + (idx + 1) * SL], T.stage[:, d * F + idx * SL:d * F + (idx + 1) * SL],
+                 T.sem["a%d" % r], T.sem.sent, pid, rid, _mask(eng))
+    sent += len(eng)
     for c in range(2):
-        d = [d for hi, d in _singles(r, c) if hi == idx][0]
-        g.wait_ge(T.sem["h%d" % c], n_on // QN)
-        sent += _block(g, core, T, topo, r, d)
+        for d in [d for hi, d in _singles(r, c) if hi == idx]:
+            g.wait_ge(T.sem["h%d" % c], n_on // QN)
+            sent += _block(g, core, T, topo, r, d)
     for hi, d0 in _pairs(r):
         if hi == idx:
             g.wait_ge(T.sem.h2, n_on // 2)
@@ -122,8 +137,9 @@ def rank_program(g, core, T, topo):
     partner = r ^ 1
     tab = [T.tab0, T.tab1, T.tab2, T.tab3]
     qs = _quarters(r)
-    col0 = [qs[0] * F, qs[1] * F, h * HN * F]
-    wid = [QN * F, QN * F, HN * F]
+    oc = _opener(r) * F
+    col0 = [qs[0] * F + F, qs[1] * F, h * HN * F]
+    wid = [(QN - 1) * F, QN * F, HN * F]
     ps = [T.ps0, T.ps1, T.ps2]
     v, pe = g.vector, g.tensor
     near = h * HN + 2 * ((q + 1) % NP)
@@ -133,7 +149,10 @@ def rank_program(g, core, T, topo):
             T.sem["l%d%d" % (c, k)], 16)
 
     for k in range(K):
-        load(g.sync, 0, k)
+        (g.sync if k % 2 else g.scalar).dma_start(tab[k][:, oc:oc + F], T.gr[k, :, oc:oc + F]).then_inc(
+            T.sem["lo%d" % k], 16)
+    for k in range(K):
+        load(g.sync if k % 2 else g.scalar, 0, k)
     v.memset(T.seed[0:1, :], 0.0).then_inc(T.sem.fillz, 1)
     v.memset(T.idb[:, :], 0.0).then_inc(T.sem.fill, 1)
     v.wait_ge(T.sem.fillz, 1)
@@ -144,6 +163,14 @@ def rank_program(g, core, T, topo):
     for c in (1, 2):
         for k in range(K):
             load(g.sync if k % 2 else g.scalar, c, k)
+
+    for i, out in enumerate((T.oa, T.ob)):
+        v.wait_ge(T.sem["lo%d" % (2 * i)], 16)
+        v.wait_ge(T.sem["lo%d" % (2 * i + 1)], 16)
+        v.tensor_tensor(out[:, :], tab[2 * i][:, oc:oc + F], tab[2 * i + 1][:, oc:oc + F],
+                        AluOpType.add).then_inc(T.sem.vo, 1)
+    v.wait_ge(T.sem.vo, 2)
+    v.tensor_tensor(T.stage[:, oc:oc + F], T.oa[:, :], T.ob[:, :], AluOpType.add).then_inc(T.sem.sto, 1)
 
     v.wait_ge(T.sem.idd, 16)
     v.tensor_copy(T.idb[32:64, 32:64], T.idb[0:32, 0:32]).then_inc(T.sem.idc1, 1)
@@ -180,19 +207,21 @@ def rank_program(g, core, T, topo):
 
     def to_helpers(items, width, deal, sem):
         trs, n = [], 0
-        for i, (hi, d0) in enumerate(items):
-            eng = all_eng[(hi if deal else i)::len(items)]
-            ap = T.stage[:, d0 * F:d0 * F + width]
+        for i, (hi, a) in enumerate(items):
+            eng = all_eng[hi::QN] if deal else all_eng[i::len(items)]
+            ap = T.stage[:, a:a + width]
             trs.append(_transfer(T, topo, core, helpers[hi], eng, sem, ap, ap))
             n += len(eng)
         g.remote_dma_fused(trs, local_sem=T.sem.sent)
         return n
 
+    g.wait_ge(T.sem.sto, 1)
+    sent += to_helpers([(hi, oc + hi * SL) for hi in range(QN)], SL, True, T.sem.ho)
     for c in range(2):
         g.wait_ge(T.sem["st%d" % c], 1)
-        sent += to_helpers(_singles(r, c), F, True, T.sem["h%d" % c])
+        sent += to_helpers([(hi, d * F) for hi, d in _singles(r, c)], F, True, T.sem["h%d" % c])
     g.wait_ge(T.sem.st2, 2)
-    sent += to_helpers(_pairs(r), PAIR, False, T.sem.h2)
+    sent += to_helpers([(hi, d * F) for hi, d in _pairs(r)], PAIR, False, T.sem.h2)
     g.wait_ge(T.sem.std, 1)
     sent += _blocks(g, core, T, topo, r, near)
     g.wait_ge(T.sem.stp, 1)
@@ -200,6 +229,8 @@ def rank_program(g, core, T, topo):
 
     def arrived(qu, s):
         n = len(_bits(topo.mask(T.cores[s], core)))
+        if _opener(s) == r:
+            n *= QN
         qu.wait_ge(T.sem["a%d" % s], n if (s == partner or s // HN != h) else n // 2)
 
     def slot(s):

from concourse.bass import DstId, RemoteDMATransfer
from concourse.mybir import AluOpType

N, K, F = 16, 4, 64
SIM_CORES = 256
HN = N // 2
QN = N // 4
PAIR = 2 * F
NP = HN // 2
SL = F // QN

SCRATCH = {
    "tab0": ("sbuf", [128, N * F], "bfloat16"),
    "tab1": ("sbuf", [128, N * F], "bfloat16"),
    "tab2": ("sbuf", [128, N * F], "bfloat16"),
    "tab3": ("sbuf", [128, N * F], "bfloat16"),
    "stage": ("sbuf", [128, N * F], "float32"),
    "land": ("sbuf", [128, N * F], "float32"),
    "seed": ("sbuf", [128, 33 * 32], "bfloat16"),
    "idb": ("sbuf", [128, 128], "bfloat16"),
    "idf": ("sbuf", [128, 128], "float32"),
    "oa": ("sbuf", [128, F], "float32"),
    "ob": ("sbuf", [128, F], "float32"),
    "two": ("sbuf", [128, F], "float32"),
    "res": ("sbuf", [128, F], "float32"),
    "ps0": ("psum", [128, 512], "float32"),
    "ps1": ("psum", [128, 512], "float32"),
    "ps2": ("psum", [128, 512], "float32"),
    "fin": ("psum", [128, 512], "float32"),
}
SEMAPHORES = (["fillz", "fill", "idd", "idc1", "idc2", "idc3", "pe0", "pe1", "pe2", "st0", "st1", "st2", "std", "stp",
               "h0", "h1", "h2", "ho", "vo", "sto", "sent", "pefin", "vtwo", "vfin", "ydone"]
              + ["l%d%d" % (c, k) for c in range(3) for k in range(K)]
              + ["lo%d" % k for k in range(K)]
              + ["a%d" % s for s in range(N)])


def _bits(mask):
    return [e for e in range(mask.bit_length()) if (mask >> e) & 1]


def _mask(engines):
    m = 0
    for e in engines:
        m |= 1 << e
    return m


def _helpers(owner, topo):
    chip = [c for c in range(SIM_CORES)
            if c != owner and topo.host(c) == topo.host(owner) and topo.chip(c) == topo.chip(owner)]
    same = [c for c in chip if topo.die(c) == topo.die(owner)]
    other = [c for c in chip if topo.die(c) != topo.die(owner)]
    return [same[0], other[0], same[1], other[1]]


def _quarters(r):
    base = (1 - r // HN) * HN
    return [base + (r % 2) * QN, base + (1 - r % 2) * QN]


def _opener(r):
    return _quarters(r)[0]


def _singles(r, c):
    return [((j + r // 2) % QN, _quarters(r)[c] + j) for j in range(1 if c == 0 else 0, QN)]


def _pairs(r):
    h, q = r // HN, (r % HN) // 2
    return [(hi, h * HN + 2 * ((q + o) % NP)) for o, hi in ((2, 1), (3, 3))]


def _transfer(T, topo, core, dst, engines, sem, src, out):
    rid, pid = topo.addr(dst, core)
    return RemoteDMATransfer(dst_ids=[DstId(rid=rid, pnc=pid)], dma_engine_mask=_mask(engines), remote_sem=sem,
                             src=src, dst=out)


def _block(g, core, T, topo, r, d):
    eng = _bits(topo.mask(core, T.cores[d]))
    rid, pid = topo.addr(T.cores[d], core)
    g.remote_dma(T.land[:, r * F:(r + 1) * F], T.stage[:, d * F:(d + 1) * F], T.sem["a%d" % r], T.sem.sent,
                 pid, rid, _mask(eng))
    return len(eng)


def _blocks(g, core, T, topo, r, d0):
    trs, n = [], 0
    for t in range(2):
        d = d0 + t
        eng = _bits(topo.mask(core, T.cores[d]))[t::2]
        trs.append(_transfer(T, topo, core, T.cores[d], eng, T.sem["a%d" % r],
                             T.stage[:, d * F:(d + 1) * F], T.land[:, r * F:(r + 1) * F]))
        n += len(eng)
    g.remote_dma_fused(trs, local_sem=T.sem.sent)
    return n


def _helper_program(g, core, T, topo, owner, idx):
    r = T.rank_of(owner)
    n_on = len(_bits(topo.mask(owner, core)))
    sent = 0
    d = _opener(r)
    eng = _bits(topo.mask(core, T.cores[d]))
    rid, pid = topo.addr(T.cores[d], core)
    g.wait_ge(T.sem.ho, n_on // QN)
    g.remote_dma(T.land[:, r * F + idx * SL:r * F + (idx + 1) * SL], T.stage[:, d * F + idx * SL:d * F + (idx + 1) * SL],
                 T.sem["a%d" % r], T.sem.sent, pid, rid, _mask(eng))
    sent += len(eng)
    for c in range(2):
        for d in [d for hi, d in _singles(r, c) if hi == idx]:
            g.wait_ge(T.sem["h%d" % c], n_on // QN)
            sent += _block(g, core, T, topo, r, d)
    for hi, d0 in _pairs(r):
        if hi == idx:
            g.wait_ge(T.sem.h2, n_on // 2)
            sent += _blocks(g, core, T, topo, r, d0)
    g.wait_ge(T.sem.sent, sent)


def rank_program(g, core, T, topo):
    owners = [c for c in T.cores if topo.host(c) == topo.host(core) and topo.chip(c) == topo.chip(core)]
    if not owners:
        return
    owner = owners[0]
    helpers = _helpers(owner, topo)
    if core != owner:
        if core in helpers:
            _helper_program(g, core, T, topo, owner, helpers.index(core))
        return

    r = T.rank_of(core)
    h = r // HN
    q = (r % HN) // 2
    partner = r ^ 1
    tab = [T.tab0, T.tab1, T.tab2, T.tab3]
    qs = _quarters(r)
    oc = _opener(r) * F
    col0 = [qs[0] * F + F, qs[1] * F, h * HN * F]
    wid = [(QN - 1) * F, QN * F, HN * F]
    ps = [T.ps0, T.ps1, T.ps2]
    v, pe = g.vector, g.tensor
    near = h * HN + 2 * ((q + 1) % NP)

    def load(qu, c, k):
        qu.dma_start(tab[k][:, col0[c]:col0[c] + wid[c]], T.gr[k, :, col0[c]:col0[c] + wid[c]]).then_inc(
            T.sem["l%d%d" % (c, k)], 16)

    for k in range(K):
        (g.sync if k % 2 else g.scalar).dma_start(tab[k][:, oc:oc + F], T.gr[k, :, oc:oc + F]).then_inc(
            T.sem["lo%d" % k], 16)
    for k in range(K):
        load(g.sync if k % 2 else g.scalar, 0, k)
    v.memset(T.seed[0:1, :], 0.0).then_inc(T.sem.fillz, 1)
    v.memset(T.idb[:, :], 0.0).then_inc(T.sem.fill, 1)
    v.wait_ge(T.sem.fillz, 1)
    v.memset(T.seed[0:1, 0:33 * 32:33], 1.0).then_inc(T.sem.fill, 1)
    g.scalar.wait_ge(T.sem.fill, 2)
    g.scalar.dma_start(T.idb[0:33, 0:32], T.seed[0:1, :]).then_inc(T.sem.idd, 16)
    g.sync.wait_ge(T.sem.fill, 2)
    for c in (1, 2):
        for k in range(K):
            load(g.sync if k % 2 else g.scalar, c, k)

    for i, out in enumerate((T.oa, T.ob)):
        v.wait_ge(T.sem["lo%d" % (2 * i)], 16)
        v.wait_ge(T.sem["lo%d" % (2 * i + 1)], 16)
        v.tensor_tensor(out[:, :], tab[2 * i][:, oc:oc + F], tab[2 * i + 1][:, oc:oc + F],
                        AluOpType.add).then_inc(T.sem.vo, 1)
    v.wait_ge(T.sem.vo, 2)
    v.tensor_tensor(T.stage[:, oc:oc + F], T.oa[:, :], T.ob[:, :], AluOpType.add).then_inc(T.sem.sto, 1)

    v.wait_ge(T.sem.idd, 16)
    v.tensor_copy(T.idb[32:64, 32:64], T.idb[0:32, 0:32]).then_inc(T.sem.idc1, 1)
    v.wait_ge(T.sem.idc1, 1)
    v.tensor_copy(T.idb[64:128, 64:128], T.idb[0:64, 0:64]).then_inc(T.sem.idc2, 1)

    pe.wait_ge(T.sem.idc2, 1)
    for c in range(3):
        for k in range(K - 1):
            pe.wait_ge(T.sem["l%d%d" % (c, k)], 16)
            mm = pe.matmul(ps[c][:, 0:wid[c]], T.idb[:, :], tab[k][:, col0[c]:col0[c] + wid[c]], k == 0, k == K - 2)
        mm.then_inc(T.sem["pe%d" % c], 1)

    def fold(c, a, n, sem):
        v.tensor_tensor(T.stage[:, a:a + n], ps[c][:, a - col0[c]:a - col0[c] + n], tab[K - 1][:, a:a + n],
                        AluOpType.add).then_inc(sem, 1)

    for c in range(2):
        v.wait_ge(T.sem["pe%d" % c], 1)
        v.wait_ge(T.sem["l%d%d" % (c, K - 1)], 16)
        fold(c, col0[c], wid[c], T.sem["st%d" % c])
        if c == 0:
            v.wait_ge(T.sem.idc2, 1)
            v.tensor_copy(T.idf[:, :], T.idb[:, :]).then_inc(T.sem.idc3, 1)
    v.wait_ge(T.sem.pe2, 1)
    v.wait_ge(T.sem["l2%d" % (K - 1)], 16)
    for hi, d0 in _pairs(r):
        fold(2, d0 * F, PAIR, T.sem.st2)
    fold(2, near * F, PAIR, T.sem.std)
    fold(2, partner * F, F, T.sem.stp)

    all_eng = _bits(topo.mask(core, helpers[0]))
    sent = 0

    def to_helpers(items, width, deal, sem):
        trs, n = [], 0
        for i, (hi, a) in enumerate(items):
            eng = all_eng[hi::QN] if deal else all_eng[i::len(items)]
            ap = T.stage[:, a:a + width]
            trs.append(_transfer(T, topo, core, helpers[hi], eng, sem, ap, ap))
            n += len(eng)
        g.remote_dma_fused(trs, local_sem=T.sem.sent)
        return n

    g.wait_ge(T.sem.sto, 1)
    sent += to_helpers([(hi, oc + hi * SL) for hi in range(QN)], SL, True, T.sem.ho)
    for c in range(2):
        g.wait_ge(T.sem["st%d" % c], 1)
        sent += to_helpers([(hi, d * F) for hi, d in _singles(r, c)], F, True, T.sem["h%d" % c])
    g.wait_ge(T.sem.st2, 2)
    sent += to_helpers([(hi, d * F) for hi, d in _pairs(r)], PAIR, False, T.sem.h2)
    g.wait_ge(T.sem.std, 1)
    sent += _blocks(g, core, T, topo, r, near)
    g.wait_ge(T.sem.stp, 1)
    sent += _block(g, core, T, topo, r, partner)

    def arrived(qu, s):
        n = len(_bits(topo.mask(T.cores[s], core)))
        if _opener(s) == r:
            n *= QN
        qu.wait_ge(T.sem["a%d" % s], n if (s == partner or s // HN != h) else n // 2)

    def slot(s):
        return T.land[:, s * F:(s + 1) * F]

    pe.wait_ge(T.sem["l2%d" % (K - 1)], 16)
    for k in range(K):
        pe.matmul(T.fin[:, 0:F], T.idb[:, :], tab[k][:, r * F:(r + 1) * F], k == 0, False)
    others = [(1 - h) * HN + (r + i) % HN for i in range(HN)]
    mine = (r // QN) * QN
    early = [s for s in others if _quarters(s)[0] == mine] + [s for s in others if _quarters(s)[0] != mine]
    late = [h * HN + 2 * ((q - o) % NP) + t for o in (1, 2, 3) for t in range(2)]
    order = early + late[0:2] + [partner] + late[2:]
    pe.wait_ge(T.sem.idc3, 1)
    for i, s in enumerate(order[:-2]):
        arrived(pe, s)
        mm = pe.matmul(T.fin[:, 0:F], T.idf[:, :], slot(s), False, i == len(order) - 3)
    mm.then_inc(T.sem.pefin, 1)

    arrived(v, order[-2])
    arrived(v, order[-1])
    v.tensor_tensor(T.two[:, :], slot(order[-2]), slot(order[-1]), AluOpType.add).then_inc(T.sem.vtwo, 1)
    v.wait_ge(T.sem.vtwo, 1)
    v.wait_ge(T.sem.pefin, 1)
    v.tensor_tensor(T.res[:, :], T.fin[:, 0:F], T.two[:, :], AluOpType.add).then_inc(T.sem.vfin, 1)
    g.sync.wait_ge(T.sem.vfin, 1)
    g.sync.dma_start(T.y[:, :], T.res[:, :]).then_inc(T.sem.ydone, 16)
    g.sync.wait_ge(T.sem.ydone, 16)
    g.wait_ge(T.sem.sent, sent)
